import numpy as np
import ml_dtypes


def mxq(x, axis, fmt="e4m3"):
    dtype, down = {"e4m3": (ml_dtypes.float8_e4m3fn, 7), "e5m2": (ml_dtypes.float8_e5m2, 14)}[fmt]
    v = np.moveaxis(np.asarray(x, np.float32).astype(ml_dtypes.bfloat16).astype(np.float64), axis, -1)
    blocks = v.reshape(v.shape[:-1] + (-1, 32))
    amax = np.abs(blocks).max(-1, keepdims=True)
    byte = np.maximum(np.where(amax > 0, np.frexp(amax)[1] - 1 + 127, 0) - down, 1)
    scale = np.exp2(byte - 127.0)
    codes = (blocks / scale).astype(np.float32).astype(dtype).astype(np.float64)
    return np.moveaxis((codes * scale).reshape(v.shape), -1, axis)


WIDE = False


def mx_kscale(k):
    if not WIDE:
        return np.ones(k)
    levels = np.array([10, -10, 5, -5, 0])
    if k % 512:
        return np.exp2(np.random.permutation(np.resize(levels, k // 32))).repeat(32)
    a = np.empty((k // 512, 16))
    for p in range(k // 512):
        a[p, :8] = np.random.permutation(np.resize(levels, 8))
        for g in range(8):
            far = levels[np.abs(levels - a[p, g]) >= 10]
            a[p, g + 8] = far[np.random.randint(len(far))]
    return np.exp2(a.ravel()).repeat(32)


def f64(x):
    return np.asarray(x).astype(np.float64)


def striped(idx):
    return np.tile(idx.reshape(-1, 16).T, (8, 1)).astype(np.uint16)


def unstriped(offs):
    return offs[:16].T.reshape(-1).astype(np.int64)


def pack_weight(w):
    k, n = w.shape
    w = f64(np.asarray(w, np.float32).astype(ml_dtypes.bfloat16)).reshape(k // 32, 32, n)
    amax = np.abs(w).max(1)
    byte = np.clip(np.where(amax > 0, np.frexp(amax)[1] - 1 + 127 - 7, 1), 1, 254)
    scaled = (w * np.exp2(127.0 - byte)[:, None, :]).reshape(k, n).astype(np.float32)
    words = np.ascontiguousarray(scaled.reshape(k // 512, 128, 4, n).transpose(0, 1, 3, 2)).astype(ml_dtypes.float8_e4m3fn).view(np.uint8)
    return words, np.ascontiguousarray(byte.astype(np.uint8).reshape(k // 512, 16, n))


def unpack_weight(words, scales):
    g, p, n, _ = words.shape
    vals = np.ascontiguousarray(words).view(ml_dtypes.float8_e4m3fn).astype(np.float64) * np.repeat(np.exp2(scales.astype(np.float64) - 127.0), 8, axis=1)[..., None]
    return vals.transpose(0, 1, 3, 2).reshape(g * 512, n)


def sigmoid(v):
    return 1.0 / (1.0 + np.exp(-np.maximum(v, -700.0)))


K, T, S, N, D, V, U = 512, 1024, 512, 128, 4, 256, 1024
P = 2 ** 7


def setup_inputs():
    n = np.random.standard_normal
    s = mx_kscale(K)[:, None]
    packed_xT = pack_weight(n((K, T)) * s)
    return {
        "x_words": packed_xT[0],
        "x_scales": packed_xT[1],
        "w1": (n((K, N)) / np.sqrt(K) / s).astype(np.float32),
        "w2": (n((K, N)) / np.sqrt(K) / s).astype(np.float32),
        "one": (np.tile(np.random.uniform(0.8, 1.0, U), (P, 1))).astype(np.float32),
        "res": ((np.random.uniform(size=(N, U)) < 0.5) * 1.0).astype(np.float32),
        "offs": striped(np.random.permutation(T)[:S]),
        "opp": striped(np.random.permutation(np.concatenate([np.arange(S), np.random.randint(0, S, U - S)]))),
        "who": striped(np.random.permutation(S)[:V]),
    }


def reference(x_words, x_scales, w1, w2, one, res, offs, opp, who):
    xq = unpack_weight(x_words, x_scales)[:, unstriped(offs)]
    yr = mxq(f64(w1), 0, "e4m3").T @ xq
    me = yr[:, unstriped(who)]
    yd = mxq(f64(w2), 0, "e4m3").T @ xq
    dev = np.log(np.exp(yd) + 1.0) + 0.3
    de = dev[:, unstriped(who)]
    dop = dev[:, unstriped(opp)]
    gw = f64(one)[:1] / (np.sqrt(0.304 * ((dop) ** 2) + 1.0))
    mo = yr[:, unstriped(opp)]
    ex = sigmoid(gw * (np.repeat(me, D, axis=1) - mo))
    gi = (((gw) ** 2) * ex) * (-1.0 * ex + 1.0)
    iv = gi.reshape(len(gi), -1, D).sum(axis=2)
    nv = ((de) ** 2) / (((de) ** 2) * iv + 1.0)
    gr = gw * (f64(res) - ex)
    return me + nv * (gr.reshape(len(gr), -1, D).sum(axis=2))

import math
from contextlib import ExitStack

import concourse.mybir as mybir
from concourse.masks import make_identity

K, T, S, N, D, V, U = 512, 1024, 512, 128, 4, 256, 1024
FLOPS = 2 * 2 * K * N * S

F32 = mybir.dt.float32
BF16 = mybir.dt.bfloat16
I32 = mybir.dt.int32
U32 = mybir.dt.uint32
U16 = mybir.dt.uint16
U8 = mybir.dt.uint8
FP8X4 = mybir.dt.float8_e4m3fn_x4
ALU = mybir.AluOpType
ACT = mybir.ActivationFunctionType
AX = mybir.AxisListType

P = 128
PACK = 4
LIST_ROWS = 16
SPARE = 16
HALVES = 2


def tile_picked_yglick_mean_p_kernel(
    tc, x_words, x_scales, w1, w2, one, res, offs, opp, who, out
):
    nc = tc.nc
    with ExitStack() as ctx:
        sb = ctx.enter_context(tc.tile_pool(name="sb", bufs=1))
        ps = ctx.enter_context(tc.psum_pool(name="ps", bufs=1))

        offs_t = sb.tile([P, S // LIST_ROWS], U16, name="offs_t")
        opp_t = sb.tile([P, U // LIST_ROWS], U16, name="opp_t")
        who_t = sb.tile([P, V // LIST_ROWS], U16, name="who_t")
        all_words = sb.tile([P, T], I32, name="all_words", align_bytes=64)
        all_scales = sb.tile([P, T], U8, name="all_scales", align_bytes=64)
        w1_raw = sb.tile([P, PACK, N], F32, name="w1_raw")
        w2_raw = sb.tile([P, PACK, N], F32, name="w2_raw")
        one_t = sb.tile([P, U], F32, name="one_t")
        res_t = sb.tile([P, U], F32, name="res_t")

        nc.vector.memset(all_scales[:].bitcast(I32), 0)
        zero = sb.tile([P, 1], F32, name="zero")
        half = sb.tile([P, 1], F32, name="half")
        unit = sb.tile([P, 1], F32, name="unit")
        tiny = sb.tile([P, 1], F32, name="tiny")
        nc.gpsimd.memset(zero[:], 0.0)
        nc.gpsimd.memset(unit[:], 1.0)
        nc.gpsimd.memset(tiny[:], 2.0**-60)

        nc.sync.dma_start(w1_raw[:], w1.rearrange("(p j) n -> p j n", j=PACK))
        nc.sync.dma_start(offs_t[:], offs)
        for q in range(4):
            nc.sync.dma_start(
                all_scales[32 * q : 32 * q + 4, :].bitcast(I32),
                x_scales[0, 4 * q : 4 * q + 4, :].bitcast(I32),
            )
        nc.sync.dma_start(w2_raw[:], w2.rearrange("(p j) n -> p j n", j=PACK))
        nc.sync.dma_start(all_words[:], x_words[0].rearrange("p n t -> p (n t)").bitcast(I32))
        nc.scalar.activation(half[:], zero[:], ACT.Sigmoid, bias=zero[:])
        nc.sync.dma_start(who_t[:], who)
        nc.sync.dma_start(opp_t[:], opp)
        nc.sync.dma_start(one_t[:], one)
        nc.sync.dma_start(res_t[:], res)

        rating = sb.tile([P, S + SPARE], F32, name="rating")
        damp = sb.tile([P, S + SPARE], F32, name="damp")
        var = sb.tile([P, S + SPARE], F32, name="var")
        for window in (rating, damp, var):
            nc.gpsimd.memset(window[:, S:], 0.0)

        identity = sb.tile([P, P], F32, name="identity")
        make_identity(nc, identity[:])
        picked = S // HALVES

        def picked_cols(h):
            return slice(h * picked, (h + 1) * picked)

        x_scale = sb.tile([P, S], U8, name="x_scale", align_bytes=64)
        x_code = [sb.tile([P, picked], U32, name="x_code%d" % h, align_bytes=64) for h in range(HALVES)]

        def pick(h):
            entries = offs_t[:, h * picked // LIST_ROWS : (h + 1) * picked // LIST_ROWS]
            nc.vector.tensor_copy(x_code[h][:], all_words[:].bitcast(U32).indirect(entries))

        def quantise(raw, name, sign, tag):
            grouped = sb.tile([P, N, PACK], BF16, name=name + "_bf", align_bytes=64)
            code = sb.tile([P, N], U32, name=name + "_code", align_bytes=64)
            scale = sb.tile([P, N], U8, name=name + "_scale", align_bytes=64, tag=tag)
            nc.scalar.activation(grouped[:], raw[:].rearrange("p j n -> p n j"), ACT.Copy, scale=sign)
            nc.vector.quantize_mx(
                out=code[:].bitcast(FP8X4), scales=scale[:], in_=grouped[:].rearrange("p n j -> p (n j)")
            )
            return code, scale

        def product(weight, name, h):
            code, scale = weight
            acc = ps.tile([P, picked], F32, name="%s%d" % (name, h))
            nc.tensor.matmul_mx(
                out=acc[:],
                lhsT=code[:].bitcast(FP8X4),
                lhsT_scale=scale[:],
                rhs=x_code[h][:].bitcast(FP8X4),
                rhs_scale=x_scale[:, picked_cols(h)],
                start=True,
                stop=True,
            )
            return acc

        nc.vector.tensor_copy(x_scale[:], all_scales[:].indirect(offs_t[:]))
        q1 = quantise(w1_raw, "w1", 1.0, "w1_scale")
        q2 = quantise(w2_raw, "w2", -1.0, "w2_scale")
        pick(0)
        pick(1)
        sig = sb.tile([P, S], F32, name="sig")
        log_sig = sb.tile([P, S], F32, name="log_sig")
        neg_yd = []
        for h in range(HALVES):
            yr = product(q1, "yr", h)
            neg_yd.append(product(q2, "neg_yd", h))
            nc.scalar.copy(rating[:, picked_cols(h)], yr[:])
            nc.scalar.activation(sig[:, picked_cols(h)], neg_yd[h][:], ACT.Sigmoid, bias=zero[:])

        games = U // HALVES
        rated = V // HALVES

        def game_cols(h):
            return slice(h * games, (h + 1) * games)

        def rated_cols(h):
            return slice(h * rated, (h + 1) * rated)

        def opp_list(h):
            return opp_t[:, h * games // LIST_ROWS : (h + 1) * games // LIST_ROWS]

        def wide(name):
            return [sb.tile([P, games], F32, name="%s%d" % (name, h)) for h in range(HALVES)]

        def narrow(name):
            return [sb.tile([P, rated], F32, name="%s%d" % (name, h)) for h in range(HALVES)]

        warm = sb.tile([P, 3], F32, name="warm")
        cut = picked + 1
        nc.scalar.activation(log_sig[:, :cut], sig[:, :cut], ACT.Ln, scale=math.exp(-0.3), bias=tiny[:])
        nc.scalar.activation(log_sig[:, cut:], sig[:, cut:], ACT.Ln, scale=math.exp(-0.3), bias=tiny[:])
        nc.scalar.activation(warm[:, 0:1], log_sig[:, S - 1 : S], ACT.Abs_reciprocal_sqrt, bias=zero[:])

        me = sb.tile([P, V], F32, name="me")
        nc.vector.tensor_copy(me[:], rating[:].indirect(who_t[:]))
        neg_me = sb.tile([P, U], F32, name="neg_me")

        EARLY = 320
        gap0_tile = sb.tile([P, EARLY + picked], F32, name="gap0")
        neg_dev0 = sb.tile([P, picked], F32, name="neg_dev0")
        neg_dev = [neg_dev0[:], gap0_tile[:, EARLY:]]
        gap = [gap0_tile[:, :games], one_t[:, game_cols(1)]]

        def gather_gap(dst, first, last):
            nc.vector.tensor_tensor(dst, rating[:].indirect(opp_t[:, first // LIST_ROWS : last // LIST_ROWS]), neg_me[:, first:last], ALU.add)

        nc.vector.tensor_scalar(neg_me[:].rearrange("p (v d) -> p v d", d=D), me[:].unsqueeze(2).to_broadcast([P, V, D]), -1.0, None, op0=ALU.mult)
        gather_gap(gap0_tile[:, :EARLY], 0, EARLY)
        for h in range(HALVES):
            nc.vector.scalar_tensor_tensor(neg_dev[h], neg_yd[h][:], -0.3, log_sig[:, picked_cols(h)], op0=ALU.add, op1=ALU.min)
        for h in range(HALVES):
            nc.vector.tensor_tensor(var[:, picked_cols(h)], neg_dev[h], neg_dev[h], ALU.mult)
        my_var = sb.tile([P, V], F32, name="my_var")
        nc.vector.tensor_copy(my_var[:], var[:].indirect(who_t[:]))
        gather_gap(gap0_tile[:, EARLY:games], EARLY, games)

        inv_dev = sb.tile([P, V], F32, name="inv_dev")
        inv_var = sb.tile([P, V], F32, name="inv_var")
        neg_inv_var = sb.tile([P, V], F32, name="neg_inv_var")
        nc.scalar.activation(damp[:, :S], var[:, :S], ACT.Abs_reciprocal_sqrt, scale=0.304, bias=unit[:])
        nc.scalar.activation(inv_dev[:], my_var[:], ACT.Abs_reciprocal_sqrt, bias=zero[:])
        nc.scalar.activation(warm[:, 1:2], inv_dev[:, 0:1], ACT.Sigmoid, bias=zero[:])

        gw = wide("gw")
        arg = wide("arg")
        ex = wide("ex")
        gw_sq = wide("gw_sq")
        off_sq = wide("off_sq")
        for h in range(HALVES):
            nc.vector.tensor_tensor(gw[h][:], damp[:].indirect(opp_list(h)), one_t[:, game_cols(h)], ALU.mult)
        nc.scalar.activation(gw_sq[0][:], gw[0][:], ACT.Square, bias=zero[:])
        nc.scalar.activation(inv_var[:], inv_dev[:], ACT.Square, bias=zero[:])
        nc.scalar.activation(neg_inv_var[:], inv_var[:], ACT.Copy, scale=-1.0)
        for h in range(HALVES):
            if h == 1:
                gather_gap(gap[1], games, U)
                nc.scalar.activation(gw_sq[1][:], gw[1][:], ACT.Square, bias=zero[:])
            nc.vector.tensor_tensor(arg[h][:], gw[h][:], gap[h], ALU.mult)
            nc.scalar.activation(ex[h][:], arg[h][:], ACT.Sigmoid, scale=-1.0, bias=zero[:])
            nc.scalar.activation(off_sq[h][:], ex[h][:], ACT.Square, scale=-1.0, bias=half[:])
        nc.scalar.activation(warm[:, 2:3], off_sq[HALVES - 1][:, 0:1], ACT.Abs_reciprocal_sqrt, bias=half[:])

        miss = [sb.tile([P, games], F32, name="miss0"), ex[1]]
        gr = wide("gr")
        neg_gi = wide("neg_gi")
        root = narrow("root")
        nv = narrow("nv")
        gr_sum = sb.tile([P, rated], F32, name="gr_sum")
        step = narrow("step")
        new = narrow("new")

        def turned_sum(acc, parts):
            for i, part in enumerate(parts):
                nc.tensor.matmul(acc, lhsT=part, rhs=identity[:], is_transpose=True, start=(i == 0), stop=(i == len(parts) - 1))

        def by_game(t):
            return [t[:].rearrange("p (v d) -> p d v", d=D)[:, d, :] for d in range(D)]

        def info(h):
            nc.vector.scalar_tensor_tensor(neg_gi[h][:], off_sq[h][:], -0.25, gw_sq[h][:], op0=ALU.add, op1=ALU.mult)
            den_t = ps.tile([P, rated], F32, name="den_t%d" % h)
            turned_sum(den_t[:], [neg_inv_var[:, rated_cols(h)]] + by_game(neg_gi[h]))
            nc.scalar.activation(root[h][:], den_t[:], ACT.Abs_reciprocal_sqrt, bias=zero[:])
            nc.scalar.activation(nv[h][:], root[h][:], ACT.Square, bias=zero[:])

        def surprise(h, cols):
            nc.vector.tensor_tensor(miss[h][:, cols], res_t[:, game_cols(h)][:, cols], ex[h][:, cols], ALU.subtract)

        def pull(h, cols):
            nc.vector.tensor_tensor(gr[h][:, cols], miss[h][:, cols], gw[h][:, cols], ALU.mult)

        surprise(0, slice(0, games))
        info(0)
        pull(0, slice(0, games))
        gr_t = ps.tile([P, rated], F32, name="gr_t")
        turned_sum(gr_t[:], by_game(gr[0]))
        info(1)
        nv_back = ps.tile([P, rated], F32, name="nv_back", tag="yr0")
        nc.tensor.transpose(nv_back[:], nv[1][:], identity[:])
        pieces = [slice(0, games // 2), slice(games // 2, games)]
        for cols in pieces:
            surprise(1, cols)
        for cols in pieces:
            pull(1, cols)
        nc.vector.tensor_tensor(step[0][:], gr_t[:], nv[0][:], ALU.mult)
        step_back = ps.tile([P, rated], F32, name="step_back")
        nc.tensor.transpose(step_back[:], step[0][:], identity[:])
        nc.vector.tensor_reduce(gr_sum[:], gr[1][:].rearrange("p (v d) -> p v d", d=D), axis=AX.X, op=ALU.add)
        nc.vector.tensor_tensor(new[0][:], step_back[:], me[:, rated_cols(0)], ALU.add)
        nc.sync.dma_start(out[:, rated_cols(0)], new[0][:])
        nc.vector.tensor_tensor(step[1][:], nv_back[:], gr_sum[:], ALU.mult)
        nc.vector.tensor_tensor(new[1][:], step[1][:], me[:, rated_cols(1)], ALU.add)
        nc.sync.dma_start(out[:, rated_cols(1)], new[1][:])
